import numpy as np
import ml_dtypes


def mxq(x, axis, fmt="e4m3"):
    dtype, down = {"e4m3": (ml_dtypes.float8_e4m3fn, 7), "e5m2": (ml_dtypes.float8_e5m2, 14)}[fmt]
    v = np.moveaxis(np.asarray(x, np.float32).astype(ml_dtypes.bfloat16).astype(np.float64), axis, -1)
    blocks = v.reshape(v.shape[:-1] + (-1, 32))
    amax = np.abs(blocks).max(-1, keepdims=True)
    byte = np.maximum(np.where(amax > 0, np.frexp(amax)[1] - 1 + 127, 0) - down, 1)
    scale = np.exp2(byte - 127.0)
    codes = (blocks / scale).astype(np.float32).astype(dtype).astype(np.float64)
    return np.moveaxis((codes * scale).reshape(v.shape), -1, axis)


WIDE = False


def mx_kscale(k):
    if not WIDE:
        return np.ones(k)
    levels = np.array([10, -10, 5, -5, 0])
    if k % 512:
        return np.exp2(np.random.permutation(np.resize(levels, k // 32))).repeat(32)
    a = np.empty((k // 512, 16))
    for p in range(k // 512):
        a[p, :8] = np.random.permutation(np.resize(levels, 8))
        for g in range(8):
            far = levels[np.abs(levels - a[p, g]) >= 10]
            a[p, g + 8] = far[np.random.randint(len(far))]
    return np.exp2(a.ravel()).repeat(32)


def f64(x):
    return np.asarray(x).astype(np.float64)


def striped(idx):
    return np.tile(np.asarray(idx).reshape(-1, 16).T, (8, 1)).astype(np.uint16)


def unstriped(offs):
    return offs[:16].T.reshape(-1).astype(np.int64)


def striped8(idx):
    return np.asarray(idx).reshape(8, -1, 16).transpose(0, 2, 1).reshape(128, -1).astype(np.uint16)


def unstriped8(offs):
    return offs.reshape(8, 16, -1).transpose(0, 2, 1).reshape(8, -1).astype(np.int64)


def pick8(x, idx, run):
    r = np.arange(len(x))
    return x[r[:, None], idx[r % (8 * run) // run]]


E2M1 = np.array([0.0, 0.5, 1.0, 1.5, 2.0, 3.0, 4.0, 6.0, -0.0, -0.5, -1.0, -1.5, -2.0, -3.0, -4.0, -6.0])


def pack_weight(w, fmt):
    k, n = w.shape
    w = f64(np.asarray(w, np.float32).astype(ml_dtypes.bfloat16)).reshape(k // 32, 32, n)
    amax = np.abs(w).max(1)
    if fmt == "e4m3":
        byte = np.frexp(amax)[1] - 1 + 127 - 7
    else:
        mant, ex = np.frexp(amax / 6.0)
        byte = np.where(mant > 0.5, ex, ex - 1) + 127
    byte = np.clip(np.where(amax > 0, byte, 1), 1, 254)
    scaled = (w * np.exp2(127.0 - byte)[:, None, :]).reshape(k, n).astype(np.float32)
    by_word = np.ascontiguousarray(scaled.reshape(k // 512, 128, 4, n).transpose(0, 1, 3, 2))
    if fmt == "e4m3":
        words = by_word.astype(ml_dtypes.float8_e4m3fn).view(np.uint8)
    else:
        c = by_word.astype(ml_dtypes.float4_e2m1fn).view(np.uint8) & 0xF
        words = (c[..., 0::2] | (c[..., 1::2] << 4)).reshape(k // 512, 128, 2 * n)
    return np.ascontiguousarray(words), np.ascontiguousarray(byte.astype(np.uint8).reshape(k // 512, 16, n))


def unpack_weight(words, scales, fmt):
    g, _, n = scales.shape
    words = np.ascontiguousarray(words).reshape(g, 128, n, -1)
    if fmt == "e4m3":
        vals = words.view(ml_dtypes.float8_e4m3fn).astype(np.float64)
    else:
        nib = np.empty((g, 128, n, 4), np.uint8)
        nib[..., 0::2] = words & 0xF
        nib[..., 1::2] = words >> 4
        vals = E2M1[nib]
    vals = vals * np.repeat(np.exp2(scales.astype(np.float64) - 127.0), 8, axis=1)[..., None]
    return vals.transpose(0, 1, 3, 2).reshape(g * 512, n)


K, J, R, T, U, C, O, S, N, Z = 512, 256, 512, 1024, 512, 512, 128, 256, 256, 1024


def setup_inputs():
    n = np.random.standard_normal
    idx = np.stack([np.random.permutation(T)[:U] for _ in range(8)])
    idx2 = np.random.permutation(U)[:J]
    idx3 = np.stack([np.random.permutation(C)[:J] for _ in range(8)])
    idx4 = np.stack([np.random.permutation(C)[:S] for _ in range(8)])
    idx5 = np.random.permutation(C)[:S]
    idx6 = np.stack([np.random.permutation(S)[:O] for _ in range(8)])
    idx7 = np.random.permutation(Z)[:N]
    fk = mx_kscale(K)
    fr = mx_kscale(R)
    wp = pack_weight(n((K, R)) * 1 / np.sqrt(K) / fk[:, None] * fr, "e2m1")
    vsp = pack_weight(n((R, Z)) * 1 / np.sqrt(R) / fr[:, None], "e4m3")
    return {
        "ta": (np.random.randint(-7, 8, (K, T)).astype(np.float64)).astype(np.float32),
        "ga": ((np.random.randint(8, 25, (K, 1)) / 64.0) * fk[:, None]).astype(np.float32),
        "gb": (np.random.uniform(0.5, 1.6, (K, 1))).astype(np.float32),
        "w_words": wp[0],
        "w_scales": wp[1],
        "sa": (np.random.uniform(0.5, 1.6, (R, 1))).astype(np.float32),
        "sb": (np.random.uniform(0.5, 1.6, (R, 1))).astype(np.float32),
        "sd": (np.random.uniform(0.5, 1.6, (R, 1))).astype(np.float32),
        "vs_words": vsp[0],
        "vs_scales": vsp[1],
        "offs": striped8(idx),
        "offs2": striped(idx2),
        "offs3": striped8(idx3),
        "offs4": striped8(idx4),
        "offs5": striped(idx5),
        "offs6": striped8(idx6),
        "offs7": striped(idx7),
    }


def reference(ta, ga, gb, w_words, w_scales, sa, sb, sd, vs_words, vs_scales, offs, offs2, offs3, offs4, offs5, offs6, offs7):
    idx = unstriped8(offs)
    idx2 = unstriped(offs2)
    idx3 = unstriped8(offs3)
    idx4 = unstriped8(offs4)
    idx5 = unstriped(offs5)
    idx6 = unstriped8(offs6)
    idx7 = unstriped(offs7)
    wu = unpack_weight(w_words, w_scales, "e2m1")
    vsu = unpack_weight(vs_words, vs_scales, "e4m3")
    xcd = pick8(f64(ta), idx, 64) * f64(ga)
    xc = xcd[:, idx2] * f64(gb)
    xcq = mxq(xc, 0, "e4m3")
    a = wu.T @ xcq
    pw = np.zeros((R, C))
    pw[np.arange(R)[:, None], idx3[np.arange(R) % 512 // 64]] = a
    pg = np.maximum(pick8(pw, idx4, 64) * f64(sa), pw[:, idx5] * f64(sb))
    hid = pick8(pg, idx6, 64) * f64(sd)
    vsidx7g = vsu[:, idx7]
    hidq = mxq(hid, 0, "e4m3")
    y = vsidx7g.T @ hidq
    return y

@@ -1,0 +1,224 @@
+from contextlib import ExitStack
+
+import concourse.mybir as mybir
+
+K, J, R, T, U, C, O, S, N, Z = 512, 256, 512, 1024, 512, 512, 128, 256, 256, 1024
+FLOPS = 2 * K * R * J + 2 * R * N * O
+
+F32 = mybir.dt.float32
+BF16 = mybir.dt.bfloat16
+I32 = mybir.dt.int32
+U32 = mybir.dt.uint32
+U16 = mybir.dt.uint16
+U8 = mybir.dt.uint8
+FP8X4 = mybir.dt.float8_e4m3fn_x4
+FP4X4 = mybir.dt.float4_e2m1fn_x4
+COPY = mybir.ActivationFunctionType.Copy
+MAX = mybir.AluOpType.max
+
+P = 128
+PACK = 4
+HALF = J // 2
+QUADRANTS = 4
+
+
+def tile_picked_respelled_plain_one_ladder_store_plain_kernel(
+    tc, ta, ga, gb, w_words, w_scales, sa, sb, sd, vs_words, vs_scales,
+    offs, offs2, offs3, offs4, offs5, offs6, offs7, out,
+):
+    nc = tc.nc
+    with ExitStack() as ctx:
+        lists = ctx.enter_context(tc.tile_pool(name="lists", bufs=1))
+        keep = ctx.enter_context(tc.tile_pool(name="keep", bufs=1))
+        psum = ctx.enter_context(tc.psum_pool(name="psum", bufs=1))
+
+        def load_list(src, name):
+            tile = lists.tile(list(src.shape), U16, name=name)
+            nc.sync.dma_start(tile[:], src)
+            return tile
+
+        def load_factor(queue, src, name):
+            tile = keep.tile([P, PACK], F32, name=name)
+            queue.dma_start(out=tile[:], in_=src.rearrange("(p t) one -> p (t one)", t=PACK))
+            return tile
+
+        def load_scale_rows(src, width, name):
+            rows = keep.tile([PACK, QUADRANTS, width // 4], I32, name=name)
+            nc.gpsimd.dma_start(out=rows[:], in_=src[0].bitcast(I32).rearrange("(q r) n -> r q n", r=PACK))
+            return rows
+
+        def spread_scale_rows(rows, width, name):
+            plane = keep.tile([P, width], U8, name=name, align_bytes=64)
+            nc.vector.memset(plane[:].bitcast(I32), 0)
+            for q in range(QUADRANTS):
+                nc.vector.tensor_copy(out=plane[32 * q : 32 * q + PACK, :].bitcast(I32), in_=rows[:, q, :])
+            return plane
+
+        def interleaved_views(grouped, planes):
+            return (
+                grouped[:].rearrange("p (c i) t -> p c t i", i=4),
+                planes[:].rearrange("p t (c i) -> p c t i", i=4),
+            )
+
+        def quantize(grouped, width, name):
+            codes = keep.tile([P, width], U32, name=name + "_codes", align_bytes=64)
+            scales = keep.tile([P, width], U8, name=name + "_scales", align_bytes=64)
+            nc.vector.quantize_mx(
+                out=codes[:].bitcast(FP8X4), scales=scales[:], in_=grouped[:].rearrange("p c t -> p (c t)")
+            )
+            return codes, scales
+
+        ta_rows = ta.rearrange("(p t) c -> t p c", t=PACK)
+
+        def load_ta(t):
+            tile = keep.tile([P, T], F32, name=f"ta{t}", tag=f"ta{t}", align_bytes=64)
+            nc.sync.dma_start(out=tile[:], in_=ta_rows[t])
+            return tile
+
+        l1 = load_list(offs, "l1")
+        ga_sb = load_factor(nc.scalar, ga, "ga_sb")
+        gb_sb = load_factor(nc.scalar, gb, "gb_sb")
+        ta_sb = [load_ta(0), load_ta(1)]
+        l2 = load_list(offs2, "l2")
+        w_raw = keep.tile([P, 2 * R], U8, name="w_raw")
+        nc.sync.dma_start(out=w_raw[:], in_=w_words[0])
+        ta_sb = ta_sb + [load_ta(2), load_ta(3)]
+        l7 = load_list(offs7, "l7")
+        l3 = load_list(offs3, "l3")
+        l4 = load_list(offs4, "l4")
+        l5 = load_list(offs5, "l5")
+        l6 = load_list(offs6, "l6")
+        vs_raw = keep.tile([P, Z], U32, name="vs_raw")
+        nc.sync.dma_start(out=vs_raw[:].bitcast(I32), in_=vs_words[0].rearrange("p n t -> p (n t)").bitcast(I32))
+        w_rows = load_scale_rows(w_scales, R, "w_rows")
+        vs_rows = load_scale_rows(vs_scales, Z, "vs_rows")
+        sa_sb = load_factor(nc.gpsimd, sa, "sa_sb")
+        sb_sb = load_factor(nc.gpsimd, sb, "sb_sb")
+        sd_sb = load_factor(nc.gpsimd, sd, "sd_sb")
+
+        pw = [keep.tile([P, C], F32, name=f"pw{t}") for t in range(PACK)]
+        for t in range(PACK):
+            nc.vector.memset(pw[t][:], 0.0)
+        w_plane = spread_scale_rows(w_rows, R, "w_plane")
+        w_dealt = keep.tile([P, 2 * R], U8, name="w_dealt", align_bytes=64)
+        nc.vector.tensor_copy(
+            out=w_dealt[:].rearrange("p (t m b) -> p t m b", t=PACK, b=2),
+            in_=w_raw[:].rearrange("p (m t b) -> p t m b", t=PACK, b=2),
+        )
+        w_dealt_scales = keep.tile([P, R], U8, name="w_dealt_scales", align_bytes=64)
+        nc.vector.tensor_copy(
+            out=w_dealt_scales[:].rearrange("p (t m) -> p t m", t=PACK),
+            in_=w_plane[:].rearrange("p (m t) -> p t m", t=PACK),
+        )
+        vs_plane = spread_scale_rows(vs_rows, Z, "vs_plane")
+        vs_picked_scales = keep.tile([P, N], U8, name="vs_picked_scales", align_bytes=64)
+        nc.vector.tensor_copy(out=vs_picked_scales[:], in_=vs_plane[:].indirect(l7[:]))
+
+        xcd = [keep.tile([P, U], F32, name=f"xcd{t}") for t in range(PACK)]
+
+        def read_slots(planes, t, h):
+            cols = slice(h * HALF // 16, (h + 1) * HALF // 16)
+            nc.scalar.activation(
+                out=planes[:, t, :], in_=xcd[t][:].indirect(l2[:, cols]), func=COPY, scale=gb_sb[:, t : t + 1]
+            )
+
+        xc_first = keep.tile([P, PACK, HALF], BF16, name="xc_first")
+        for t in range(PACK):
+            nc.scalar.activation(
+                out=xcd[t][:], in_=ta_sb[t][:].indirect(l1[:]), func=COPY, scale=ga_sb[:, t : t + 1]
+            )
+            read_slots(xc_first, t, 0)
+
+        def first_product(codes, scales, t, bank_cols):
+            nc.tensor.matmul_mx(
+                out=bank_cols,
+                lhsT=w_dealt[:, 2 * P * t : 2 * P * (t + 1)].bitcast(FP4X4),
+                lhsT_scale=w_dealt_scales[:, P * t : P * (t + 1)],
+                rhs=codes[:].bitcast(FP8X4),
+                rhs_scale=scales[:],
+                start=True,
+                stop=True,
+            )
+
+        early = (0, 1)
+        late = (2, 3)
+        half_banks = {(t, h): psum.tile([P, HALF], F32, name=f"a{t}{h}") for t in early for h in (0, 1)}
+        whole_banks = {t: psum.tile([P, J], F32, name=f"a{t}") for t in late}
+
+        def products(codes, scales, h):
+            for t in early:
+                first_product(codes, scales, t, half_banks[t, h][:])
+            for t in late:
+                first_product(codes, scales, t, whole_banks[t][:, h * HALF : (h + 1) * HALF])
+
+        def scatter(t, values, first, count):
+            cols = slice(first // 16, (first + count) // 16)
+            nc.vector.tensor_copy(out=pw[t][:].indirect(l3[:, cols]), in_=values[:])
+
+        grouped_first = keep.tile([P, HALF, PACK], BF16, name="grouped_first", align_bytes=64)
+        dst, src = interleaved_views(grouped_first, xc_first)
+        nc.vector.tensor_copy(out=dst, in_=src)
+        products(*quantize(grouped_first, HALF, "xq_first"), 0)
+        a00 = keep.tile([P, HALF], F32, name="a00_sb")
+        nc.vector.tensor_copy(out=a00[:], in_=half_banks[0, 0][:])
+        scatter(0, a00, 0, HALF)
+
+        xc_second = keep.tile([P, PACK, HALF], BF16, name="xc_second", tag="ta3", align_bytes=64)
+        for t in range(PACK):
+            read_slots(xc_second, t, 1)
+        grouped_second = keep.tile([P, HALF, PACK], BF16, name="grouped_second", align_bytes=64)
+        dst, src = interleaved_views(grouped_second, xc_second)
+        nc.scalar.copy(out=dst, in_=src)
+        products(*quantize(grouped_second, HALF, "xq_second"), 1)
+
+        a10 = keep.tile([P, HALF], F32, name="a10_sb", tag="ta3", align_bytes=64)
+        nc.scalar.copy(out=a10[:], in_=half_banks[1, 0][:])
+        scatter(1, a10, 0, HALF)
+        for t in early:
+            a_sb = keep.tile([P, HALF], F32, name=f"a{t}1_sb")
+            nc.scalar.copy(out=a_sb[:], in_=half_banks[t, 1][:])
+            scatter(t, a_sb, HALF, HALF)
+        for t in late:
+            a_sb = keep.tile([P, J], F32, name=f"a{t}_sb", tag=f"a{t}_sb", align_bytes=64)
+            nc.scalar.copy(out=a_sb[:], in_=whole_banks[t][:])
+            scatter(t, a_sb, 0, J)
+
+        vs_picked = keep.tile([P, N], U32, name="vs_picked", tag="a3_sb", align_bytes=64)
+        nc.vector.tensor_copy(out=vs_picked[:], in_=vs_raw[:].indirect(l7[:]))
+
+        pg = [keep.tile([P, S], F32, name=f"pg{t}") for t in range(PACK)]
+        for t in range(PACK):
+            own = keep.tile([P, S], F32, name=f"own{t}")
+            shared = keep.tile([P, S], F32, name=f"shared{t}")
+            nc.scalar.activation(out=own[:], in_=pw[t][:].indirect(l4[:]), func=COPY, scale=sa_sb[:, t : t + 1])
+            nc.scalar.activation(out=shared[:], in_=pw[t][:].indirect(l5[:]), func=COPY, scale=sb_sb[:, t : t + 1])
+            nc.vector.tensor_tensor(out=pg[t][:], in0=own[:], in1=shared[:], op=MAX)
+        hid = keep.tile([P, PACK, O], BF16, name="hid")
+        for t in range(PACK):
+            nc.scalar.activation(
+                out=hid[:, t, :], in_=pg[t][:].indirect(l6[:]), func=COPY, scale=sd_sb[:, t : t + 1]
+            )
+        grouped_hid = keep.tile([P, O, PACK], BF16, name="grouped_hid", align_bytes=64)
+        dst, src = interleaved_views(grouped_hid, hid)
+        nc.vector.tensor_copy(out=dst, in_=src)
+        hid_codes, hid_scales = quantize(grouped_hid, O, "hq")
+
+        for i in range(N // P):
+            cols = slice(i * P, (i + 1) * P)
+            bank = psum.tile([P, O], F32, name=f"y{i}")
+            nc.tensor.matmul_mx(
+                out=bank[:],
+                lhsT=vs_picked[:, cols].bitcast(FP8X4),
+                lhsT_scale=vs_picked_scales[:, cols],
+                rhs=hid_codes[:].bitcast(FP8X4),
+                rhs_scale=hid_scales[:],
+                start=True,
+                stop=True,
+            )
+            y_sb = keep.tile([P, O], F32, name=f"y{i}_sb")
+            if i == 0:
+                nc.vector.tensor_copy(out=y_sb[:], in_=bank[:])
+                nc.sync.dma_start(out=out[cols, :], in_=y_sb[:])
+            else:
+                nc.scalar.copy(out=y_sb[:], in_=bank[:])
+                nc.scalar.dma_start(out=out[cols, :], in_=y_sb[:])

@@ -75,6 +75,11 @@ def tile_picked_respelled_plain_one_ladder_store_plain_kernel(
             nc.sync.dma_start(out=tile[:], in_=ta_rows[t])
             return tile
 
+        warm_in = keep.tile([P, 1], F32, name="warm_in")
+        warm_out = keep.tile([P, 1], F32, name="warm_out")
+        nc.vector.memset(warm_in[:], 0.0)
+        nc.scalar.activation(out=warm_out[:], in_=warm_in[:], func=COPY)
+
         l1 = load_list(offs, "l1")
         ga_sb = load_factor(nc.scalar, ga, "ga_sb")
         gb_sb = load_factor(nc.scalar, gb, "gb_sb")

@@ -57,7 +57,7 @@ def tile_picked_respelled_plain_one_ladder_store_plain_kernel(
         def interleaved_views(grouped, planes):
             return (
                 grouped[:].rearrange("p (c i) t -> p c t i", i=4),
-                planes[:].rearrange("p t (c i) -> p c t i", i=4),
+                planes.rearrange("p t (c i) -> p c t i", i=4),
             )
 
         def quantize(grouped, width, name):
@@ -77,17 +77,28 @@ def tile_picked_respelled_plain_one_ladder_store_plain_kernel(
 
         warm_in = keep.tile([P, 1], F32, name="warm_in")
         warm_out = keep.tile([P, 1], F32, name="warm_out")
-        nc.vector.memset(warm_in[:], 0.0)
+        nc.gpsimd.memset(warm_in[:], 0.0)
         nc.scalar.activation(out=warm_out[:], in_=warm_in[:], func=COPY)
 
+        gb_cols = gb.rearrange("(p t) one -> p (t one)", t=PACK)
+
+        def load_gb(queue, first, count):
+            tile = keep.tile([P, count], F32, name=f"gb{first}")
+            queue.dma_start(out=tile[:], in_=gb_cols[:, first : first + count])
+            return [tile[:, i : i + 1] for i in range(count)]
+
+        ta_sb = [load_ta(0)]
         l1 = load_list(offs, "l1")
-        ga_sb = load_factor(nc.scalar, ga, "ga_sb")
-        gb_sb = load_factor(nc.scalar, gb, "gb_sb")
-        ta_sb = [load_ta(0), load_ta(1)]
+        ga_sb = load_factor(nc.sync, ga, "ga_sb")
+        ta_sb.append(load_ta(1))
         l2 = load_list(offs2, "l2")
+        gb_sb = load_gb(nc.sync, 0, 1)
         w_raw = keep.tile([P, 2 * R], U8, name="w_raw")
         nc.sync.dma_start(out=w_raw[:], in_=w_words[0])
-        ta_sb = ta_sb + [load_ta(2), load_ta(3)]
+        ta_sb.append(load_ta(2))
+        gb_sb.extend(load_gb(nc.sync, 1, 1))
+        ta_sb.append(load_ta(3))
+        gb_sb.extend(load_gb(nc.sync, 2, 2))
         l7 = load_list(offs7, "l7")
         l3 = load_list(offs3, "l3")
         l4 = load_list(offs4, "l4")
@@ -107,13 +118,13 @@ def tile_picked_respelled_plain_one_ladder_store_plain_kernel(
         w_plane = spread_scale_rows(w_rows, R, "w_plane")
         w_dealt = keep.tile([P, 2 * R], U8, name="w_dealt", align_bytes=64)
         nc.vector.tensor_copy(
-            out=w_dealt[:].rearrange("p (t m b) -> p t m b", t=PACK, b=2),
-            in_=w_raw[:].rearrange("p (m t b) -> p t m b", t=PACK, b=2),
+            out=w_dealt[:].rearrange("p (t c i b) -> p c t i b", t=PACK, i=8, b=2),
+            in_=w_raw[:].rearrange("p (c i t b) -> p c t i b", t=PACK, i=8, b=2),
         )
         w_dealt_scales = keep.tile([P, R], U8, name="w_dealt_scales", align_bytes=64)
         nc.vector.tensor_copy(
-            out=w_dealt_scales[:].rearrange("p (t m) -> p t m", t=PACK),
-            in_=w_plane[:].rearrange("p (m t) -> p t m", t=PACK),
+            out=w_dealt_scales[:].rearrange("p (t c i) -> p c t i", t=PACK, i=16),
+            in_=w_plane[:].rearrange("p (c i t) -> p c t i", t=PACK, i=16),
         )
         vs_plane = spread_scale_rows(vs_rows, Z, "vs_plane")
         vs_picked_scales = keep.tile([P, N], U8, name="vs_picked_scales", align_bytes=64)
@@ -123,15 +134,14 @@ def tile_picked_respelled_plain_one_ladder_store_plain_kernel(
 
         def read_slots(planes, t, h):
             cols = slice(h * HALF // 16, (h + 1) * HALF // 16)
-            nc.scalar.activation(
-                out=planes[:, t, :], in_=xcd[t][:].indirect(l2[:, cols]), func=COPY, scale=gb_sb[:, t : t + 1]
-            )
+            nc.scalar.activation(out=planes[:, t, :], in_=xcd[t][:].indirect(l2[:, cols]), func=COPY, scale=gb_sb[t])
 
-        xc_first = keep.tile([P, PACK, HALF], BF16, name="xc_first")
         for t in range(PACK):
             nc.scalar.activation(
                 out=xcd[t][:], in_=ta_sb[t][:].indirect(l1[:]), func=COPY, scale=ga_sb[:, t : t + 1]
             )
+        xc_first = keep.tile([P, PACK, HALF], BF16, name="xc_first")
+        for t in range(PACK):
             read_slots(xc_first, t, 0)
 
         def first_product(codes, scales, t, bank_cols):
@@ -160,29 +170,24 @@ def tile_picked_respelled_plain_one_ladder_store_plain_kernel(
             cols = slice(first // 16, (first + count) // 16)
             nc.vector.tensor_copy(out=pw[t][:].indirect(l3[:, cols]), in_=values[:])
 
-        grouped_first = keep.tile([P, HALF, PACK], BF16, name="grouped_first", align_bytes=64)
-        dst, src = interleaved_views(grouped_first, xc_first)
-        nc.vector.tensor_copy(out=dst, in_=src)
-        products(*quantize(grouped_first, HALF, "xq_first"), 0)
-        a00 = keep.tile([P, HALF], F32, name="a00_sb")
-        nc.vector.tensor_copy(out=a00[:], in_=half_banks[0, 0][:])
-        scatter(0, a00, 0, HALF)
+        def interleave_pair(grouped, planes, first):
+            nc.vector.tensor_copy(
+                out=grouped[:, :, first : first + 2], in_=planes[:, first : first + 2, :].rearrange("p t c -> p c t")
+            )
 
         xc_second = keep.tile([P, PACK, HALF], BF16, name="xc_second", tag="ta3", align_bytes=64)
         for t in range(PACK):
             read_slots(xc_second, t, 1)
-        grouped_second = keep.tile([P, HALF, PACK], BF16, name="grouped_second", align_bytes=64)
-        dst, src = interleaved_views(grouped_second, xc_second)
-        nc.scalar.copy(out=dst, in_=src)
-        products(*quantize(grouped_second, HALF, "xq_second"), 1)
-
-        a10 = keep.tile([P, HALF], F32, name="a10_sb", tag="ta3", align_bytes=64)
-        nc.scalar.copy(out=a10[:], in_=half_banks[1, 0][:])
-        scatter(1, a10, 0, HALF)
-        for t in early:
-            a_sb = keep.tile([P, HALF], F32, name=f"a{t}1_sb")
-            nc.scalar.copy(out=a_sb[:], in_=half_banks[t, 1][:])
-            scatter(t, a_sb, HALF, HALF)
+        for h, planes in enumerate((xc_first, xc_second)):
+            grouped = keep.tile([P, HALF, PACK], BF16, name=f"grouped{h}", tag="grouped", align_bytes=64)
+            interleave_pair(grouped, planes, 0)
+            interleave_pair(grouped, planes, 2)
+            products(*quantize(grouped, HALF, f"xq{h}"), h)
+        for h in (0, 1):
+            for t in early:
+                a_sb = keep.tile([P, HALF], F32, name=f"a{t}{h}_sb")
+                nc.scalar.copy(out=a_sb[:], in_=half_banks[t, h][:])
+                scatter(t, a_sb, h * HALF, HALF)
         for t in late:
             a_sb = keep.tile([P, J], F32, name=f"a{t}_sb", tag=f"a{t}_sb", align_bytes=64)
             nc.scalar.copy(out=a_sb[:], in_=whole_banks[t][:])
@@ -199,14 +204,33 @@ def tile_picked_respelled_plain_one_ladder_store_plain_kernel(
             nc.scalar.activation(out=shared[:], in_=pw[t][:].indirect(l5[:]), func=COPY, scale=sb_sb[:, t : t + 1])
             nc.vector.tensor_tensor(out=pg[t][:], in0=own[:], in1=shared[:], op=MAX)
         hid = keep.tile([P, PACK, O], BF16, name="hid")
-        for t in range(PACK):
+
+        def read_places(t, first, count):
             nc.scalar.activation(
-                out=hid[:, t, :], in_=pg[t][:].indirect(l6[:]), func=COPY, scale=sd_sb[:, t : t + 1]
+                out=hid[:, t, first : first + count],
+                in_=pg[t][:].indirect(l6[:, first // 16 : (first + count) // 16]),
+                func=COPY,
+                scale=sd_sb[:, t : t + 1],
             )
+
+        for t in range(PACK - 1):
+            read_places(t, 0, O)
         grouped_hid = keep.tile([P, O, PACK], BF16, name="grouped_hid", align_bytes=64)
-        dst, src = interleaved_views(grouped_hid, hid)
-        nc.vector.tensor_copy(out=dst, in_=src)
-        hid_codes, hid_scales = quantize(grouped_hid, O, "hq")
+        hid_codes = keep.tile([P, O], U32, name="hid_codes", align_bytes=64)
+        hid_scales = keep.tile([P, O], U8, name="hid_scales", align_bytes=64)
+        halves = [slice(0, O // 2), slice(O // 2, O)]
+        for cols in halves:
+            read_places(PACK - 1, cols.start, O // 2)
+            nc.vector.tensor_copy(
+                out=grouped_hid[:, cols, :].rearrange("p (c i) t -> p c t i", i=4),
+                in_=hid[:, :, cols].rearrange("p t (c i) -> p c t i", i=4),
+            )
+        for cols in halves:
+            nc.vector.quantize_mx(
+                out=hid_codes[:, cols].bitcast(FP8X4),
+                scales=hid_scales[:, cols],
+                in_=grouped_hid[:, cols, :].rearrange("p c t -> p (c t)"),
+            )
 
         for i in range(N // P):
             cols = slice(i * P, (i + 1) * P)

@@ -44,7 +44,7 @@ def tile_picked_respelled_plain_one_ladder_store_plain_kernel(
 
         def load_scale_rows(src, width, name):
             rows = keep.tile([PACK, QUADRANTS, width // 4], I32, name=name)
-            nc.gpsimd.dma_start(out=rows[:], in_=src[0].bitcast(I32).rearrange("(q r) n -> r q n", r=PACK))
+            nc.scalar.dma_start(out=rows[:], in_=src[0].bitcast(I32).rearrange("(q r) n -> r q n", r=PACK))
             return rows
 
         def spread_scale_rows(rows, width, name):
@@ -77,37 +77,26 @@ def tile_picked_respelled_plain_one_ladder_store_plain_kernel(
 
         warm_in = keep.tile([P, 1], F32, name="warm_in")
         warm_out = keep.tile([P, 1], F32, name="warm_out")
-        nc.gpsimd.memset(warm_in[:], 0.0)
+        nc.vector.memset(warm_in[:], 0.0)
         nc.scalar.activation(out=warm_out[:], in_=warm_in[:], func=COPY)
 
-        gb_cols = gb.rearrange("(p t) one -> p (t one)", t=PACK)
-
-        def load_gb(queue, first, count):
-            tile = keep.tile([P, count], F32, name=f"gb{first}")
-            queue.dma_start(out=tile[:], in_=gb_cols[:, first : first + count])
-            return [tile[:, i : i + 1] for i in range(count)]
-
-        ta_sb = [load_ta(0)]
         l1 = load_list(offs, "l1")
-        ga_sb = load_factor(nc.sync, ga, "ga_sb")
-        ta_sb.append(load_ta(1))
+        ga_sb = load_factor(nc.scalar, ga, "ga_sb")
+        w_rows = load_scale_rows(w_scales, R, "w_rows")
+        vs_rows = load_scale_rows(vs_scales, Z, "vs_rows")
+        ta_sb = [load_ta(0), load_ta(1), load_ta(2)]
         l2 = load_list(offs2, "l2")
-        gb_sb = load_gb(nc.sync, 0, 1)
+        l7 = load_list(offs7, "l7")
         w_raw = keep.tile([P, 2 * R], U8, name="w_raw")
         nc.sync.dma_start(out=w_raw[:], in_=w_words[0])
-        ta_sb.append(load_ta(2))
-        gb_sb.extend(load_gb(nc.sync, 1, 1))
         ta_sb.append(load_ta(3))
-        gb_sb.extend(load_gb(nc.sync, 2, 2))
-        l7 = load_list(offs7, "l7")
         l3 = load_list(offs3, "l3")
         l4 = load_list(offs4, "l4")
         l5 = load_list(offs5, "l5")
         l6 = load_list(offs6, "l6")
         vs_raw = keep.tile([P, Z], U32, name="vs_raw")
         nc.sync.dma_start(out=vs_raw[:].bitcast(I32), in_=vs_words[0].rearrange("p n t -> p (n t)").bitcast(I32))
-        w_rows = load_scale_rows(w_scales, R, "w_rows")
-        vs_rows = load_scale_rows(vs_scales, Z, "vs_rows")
+        gb_sb = load_factor(nc.gpsimd, gb, "gb_sb")
         sa_sb = load_factor(nc.gpsimd, sa, "sa_sb")
         sb_sb = load_factor(nc.gpsimd, sb, "sb_sb")
         sd_sb = load_factor(nc.gpsimd, sd, "sd_sb")
@@ -134,7 +123,7 @@ def tile_picked_respelled_plain_one_ladder_store_plain_kernel(
 
         def read_slots(planes, t, h):
             cols = slice(h * HALF // 16, (h + 1) * HALF // 16)
-            nc.scalar.activation(out=planes[:, t, :], in_=xcd[t][:].indirect(l2[:, cols]), func=COPY, scale=gb_sb[t])
+            nc.scalar.activation(out=planes[:, t, :], in_=xcd[t][:].indirect(l2[:, cols]), func=COPY, scale=gb_sb[:, t : t + 1])
 
         for t in range(PACK):
             nc.scalar.activation(
@@ -170,18 +159,13 @@ def tile_picked_respelled_plain_one_ladder_store_plain_kernel(
             cols = slice(first // 16, (first + count) // 16)
             nc.vector.tensor_copy(out=pw[t][:].indirect(l3[:, cols]), in_=values[:])
 
-        def interleave_pair(grouped, planes, first):
-            nc.vector.tensor_copy(
-                out=grouped[:, :, first : first + 2], in_=planes[:, first : first + 2, :].rearrange("p t c -> p c t")
-            )
-
         xc_second = keep.tile([P, PACK, HALF], BF16, name="xc_second", tag="ta3", align_bytes=64)
         for t in range(PACK):
             read_slots(xc_second, t, 1)
         for h, planes in enumerate((xc_first, xc_second)):
             grouped = keep.tile([P, HALF, PACK], BF16, name=f"grouped{h}", tag="grouped", align_bytes=64)
-            interleave_pair(grouped, planes, 0)
-            interleave_pair(grouped, planes, 2)
+            dst, src = interleaved_views(grouped, planes[:])
+            nc.vector.tensor_copy(out=dst, in_=src)
             products(*quantize(grouped, HALF, f"xq{h}"), h)
         for h in (0, 1):
             for t in early:

@@ -18,8 +18,12 @@ MAX = mybir.AluOpType.max
 
 P = 128
 PACK = 4
-HALF = J // 2
 QUADRANTS = 4
+PER_COLUMN = 16
+HALF = J // 2
+RUN = 4
+EARLY = (0, 1)
+LATE = (2, 3)
 
 
 def tile_picked_respelled_plain_one_ladder_store_plain_kernel(
@@ -37,6 +41,9 @@ def tile_picked_respelled_plain_one_ladder_store_plain_kernel(
             nc.sync.dma_start(tile[:], src)
             return tile
 
+        def entries(list_tile, first, count):
+            return list_tile[:, first // PER_COLUMN : (first + count) // PER_COLUMN]
+
         def load_factor(queue, src, name):
             tile = keep.tile([P, PACK], F32, name=name)
             queue.dma_start(out=tile[:], in_=src.rearrange("(p t) one -> p (t one)", t=PACK))
@@ -48,31 +55,29 @@ def tile_picked_respelled_plain_one_ladder_store_plain_kernel(
             return rows
 
         def spread_scale_rows(rows, width, name):
-            plane = keep.tile([P, width], U8, name=name, align_bytes=64)
-            nc.vector.memset(plane[:].bitcast(I32), 0)
+            spread = keep.tile([P, width], U8, name=name, align_bytes=64)
+            nc.vector.memset(spread[:].bitcast(I32), 0)
             for q in range(QUADRANTS):
-                nc.vector.tensor_copy(out=plane[32 * q : 32 * q + PACK, :].bitcast(I32), in_=rows[:, q, :])
-            return plane
+                nc.vector.tensor_copy(out=spread[32 * q : 32 * q + PACK, :].bitcast(I32), in_=rows[:, q, :])
+            return spread
 
-        def interleaved_views(grouped, planes):
-            return (
-                grouped[:].rearrange("p (c i) t -> p c t i", i=4),
-                planes.rearrange("p t (c i) -> p c t i", i=4),
+        def interleave(grouped, planes):
+            nc.vector.tensor_copy(
+                out=grouped.rearrange("p (c i) t -> p c t i", i=RUN),
+                in_=planes.rearrange("p t (c i) -> p c t i", i=RUN),
             )
 
-        def quantize(grouped, width, name):
-            codes = keep.tile([P, width], U32, name=name + "_codes", align_bytes=64)
-            scales = keep.tile([P, width], U8, name=name + "_scales", align_bytes=64)
-            nc.vector.quantize_mx(
-                out=codes[:].bitcast(FP8X4), scales=scales[:], in_=grouped[:].rearrange("p c t -> p (c t)")
-            )
-            return codes, scales
+        def quantize(codes, scales, grouped):
+            nc.vector.quantize_mx(out=codes.bitcast(FP8X4), scales=scales, in_=grouped.rearrange("p c t -> p (c t)"))
 
-        ta_rows = ta.rearrange("(p t) c -> t p c", t=PACK)
+        def scaled_gather(dst, window, offsets, factor, t):
+            nc.scalar.activation(out=dst, in_=window[:].indirect(offsets), func=COPY, scale=factor[:, t : t + 1])
+
+        ta_planes = ta.rearrange("(p t) c -> t p c", t=PACK)
 
         def load_ta(t):
             tile = keep.tile([P, T], F32, name=f"ta{t}", tag=f"ta{t}", align_bytes=64)
-            nc.sync.dma_start(out=tile[:], in_=ta_rows[t])
+            nc.sync.dma_start(out=tile[:], in_=ta_planes[t])
             return tile
 
         warm_in = keep.tile([P, 1], F32, name="warm_in")
@@ -80,158 +85,130 @@ def tile_picked_respelled_plain_one_ladder_store_plain_kernel(
         nc.vector.memset(warm_in[:], 0.0)
         nc.scalar.activation(out=warm_out[:], in_=warm_in[:], func=COPY)
 
-        l1 = load_list(offs, "l1")
+        ta_sb = [load_ta(0)]
+        word_list = load_list(offs, "word_list")
         ga_sb = load_factor(nc.scalar, ga, "ga_sb")
         w_rows = load_scale_rows(w_scales, R, "w_rows")
         vs_rows = load_scale_rows(vs_scales, Z, "vs_rows")
-        ta_sb = [load_ta(0), load_ta(1), load_ta(2)]
-        l2 = load_list(offs2, "l2")
-        l7 = load_list(offs7, "l7")
+        gb_sb = load_factor(nc.gpsimd, gb, "gb_sb")
+        ta_sb.extend([load_ta(1), load_ta(2)])
+        slot_list = load_list(offs2, "slot_list")
+        ta_sb.append(load_ta(3))
         w_raw = keep.tile([P, 2 * R], U8, name="w_raw")
         nc.sync.dma_start(out=w_raw[:], in_=w_words[0])
-        ta_sb.append(load_ta(3))
-        l3 = load_list(offs3, "l3")
-        l4 = load_list(offs4, "l4")
-        l5 = load_list(offs5, "l5")
-        l6 = load_list(offs6, "l6")
+        store_list = load_list(offs7, "store_list")
+        board_list = load_list(offs3, "board_list")
+        own_list = load_list(offs4, "own_list")
+        shared_list = load_list(offs5, "shared_list")
+        sa_sb = load_factor(nc.sync, sa, "sa_sb")
+        sb_sb = load_factor(nc.sync, sb, "sb_sb")
+        place_list = load_list(offs6, "place_list")
+        sd_sb = load_factor(nc.sync, sd, "sd_sb")
         vs_raw = keep.tile([P, Z], U32, name="vs_raw")
         nc.sync.dma_start(out=vs_raw[:].bitcast(I32), in_=vs_words[0].rearrange("p n t -> p (n t)").bitcast(I32))
-        gb_sb = load_factor(nc.gpsimd, gb, "gb_sb")
-        sa_sb = load_factor(nc.gpsimd, sa, "sa_sb")
-        sb_sb = load_factor(nc.gpsimd, sb, "sb_sb")
-        sd_sb = load_factor(nc.gpsimd, sd, "sd_sb")
 
         pw = [keep.tile([P, C], F32, name=f"pw{t}") for t in range(PACK)]
         for t in range(PACK):
             nc.vector.memset(pw[t][:], 0.0)
-        w_plane = spread_scale_rows(w_rows, R, "w_plane")
+
+        w_spread = spread_scale_rows(w_rows, R, "w_spread")
         w_dealt = keep.tile([P, 2 * R], U8, name="w_dealt", align_bytes=64)
         nc.vector.tensor_copy(
-            out=w_dealt[:].rearrange("p (t c i b) -> p c t i b", t=PACK, i=8, b=2),
-            in_=w_raw[:].rearrange("p (c i t b) -> p c t i b", t=PACK, i=8, b=2),
+            out=w_dealt[:].bitcast(U16).rearrange("p (t c i) -> p c t i", t=PACK, i=8),
+            in_=w_raw[:].bitcast(U16).rearrange("p (c i t) -> p c t i", t=PACK, i=8),
         )
         w_dealt_scales = keep.tile([P, R], U8, name="w_dealt_scales", align_bytes=64)
         nc.vector.tensor_copy(
             out=w_dealt_scales[:].rearrange("p (t c i) -> p c t i", t=PACK, i=16),
-            in_=w_plane[:].rearrange("p (c i t) -> p c t i", t=PACK, i=16),
+            in_=w_spread[:].rearrange("p (c i t) -> p c t i", t=PACK, i=16),
         )
-        vs_plane = spread_scale_rows(vs_rows, Z, "vs_plane")
-        vs_picked_scales = keep.tile([P, N], U8, name="vs_picked_scales", align_bytes=64)
-        nc.vector.tensor_copy(out=vs_picked_scales[:], in_=vs_plane[:].indirect(l7[:]))
+        vs_spread = spread_scale_rows(vs_rows, Z, "vs_spread")
 
         xcd = [keep.tile([P, U], F32, name=f"xcd{t}") for t in range(PACK)]
-
-        def read_slots(planes, t, h):
-            cols = slice(h * HALF // 16, (h + 1) * HALF // 16)
-            nc.scalar.activation(out=planes[:, t, :], in_=xcd[t][:].indirect(l2[:, cols]), func=COPY, scale=gb_sb[:, t : t + 1])
-
         for t in range(PACK):
-            nc.scalar.activation(
-                out=xcd[t][:], in_=ta_sb[t][:].indirect(l1[:]), func=COPY, scale=ga_sb[:, t : t + 1]
-            )
-        xc_first = keep.tile([P, PACK, HALF], BF16, name="xc_first")
+            scaled_gather(xcd[t][:], ta_sb[t], word_list[:], ga_sb, t)
+        xc_first = keep.tile([P, PACK, HALF], BF16, name="xc_first", tag="xc_first", align_bytes=64)
         for t in range(PACK):
-            read_slots(xc_first, t, 0)
+            scaled_gather(xc_first[:, t, :], xcd[t], entries(slot_list, 0, HALF), gb_sb, t)
 
-        def first_product(codes, scales, t, bank_cols):
-            nc.tensor.matmul_mx(
-                out=bank_cols,
-                lhsT=w_dealt[:, 2 * P * t : 2 * P * (t + 1)].bitcast(FP4X4),
-                lhsT_scale=w_dealt_scales[:, P * t : P * (t + 1)],
-                rhs=codes[:].bitcast(FP8X4),
-                rhs_scale=scales[:],
-                start=True,
-                stop=True,
-            )
-
-        early = (0, 1)
-        late = (2, 3)
-        half_banks = {(t, h): psum.tile([P, HALF], F32, name=f"a{t}{h}") for t in early for h in (0, 1)}
-        whole_banks = {t: psum.tile([P, J], F32, name=f"a{t}") for t in late}
-
-        def products(codes, scales, h):
-            for t in early:
-                first_product(codes, scales, t, half_banks[t, h][:])
-            for t in late:
-                first_product(codes, scales, t, whole_banks[t][:, h * HALF : (h + 1) * HALF])
-
-        def scatter(t, values, first, count):
-            cols = slice(first // 16, (first + count) // 16)
-            nc.vector.tensor_copy(out=pw[t][:].indirect(l3[:, cols]), in_=values[:])
+        half_banks = {(t, h): psum.tile([P, HALF], F32, name=f"a{t}{h}") for t in EARLY for h in (0, 1)}
+        whole_banks = {t: psum.tile([P, J], F32, name=f"a{t}") for t in LATE}
 
         xc_second = keep.tile([P, PACK, HALF], BF16, name="xc_second", tag="ta3", align_bytes=64)
         for t in range(PACK):
-            read_slots(xc_second, t, 1)
-        for h, planes in enumerate((xc_first, xc_second)):
+            scaled_gather(xc_second[:, t, :], xcd[t], entries(slot_list, HALF, HALF), gb_sb, t)
+
+        def first_product(xc_half, h):
             grouped = keep.tile([P, HALF, PACK], BF16, name=f"grouped{h}", tag="grouped", align_bytes=64)
-            dst, src = interleaved_views(grouped, planes[:])
-            nc.vector.tensor_copy(out=dst, in_=src)
-            products(*quantize(grouped, HALF, f"xq{h}"), h)
+            interleave(grouped[:], xc_half[:])
+            codes = keep.tile([P, HALF], U32, name=f"xq{h}_codes", align_bytes=64)
+            scales = keep.tile([P, HALF], U8, name=f"xq{h}_scales", align_bytes=64)
+            quantize(codes[:], scales[:], grouped[:])
+            for t in EARLY + LATE:
+                nc.tensor.matmul_mx(
+                    out=half_banks[t, h][:] if t in EARLY else whole_banks[t][:, h * HALF : (h + 1) * HALF],
+                    lhsT=w_dealt[:, 2 * P * t : 2 * P * (t + 1)].bitcast(FP4X4),
+                    lhsT_scale=w_dealt_scales[:, P * t : P * (t + 1)],
+                    rhs=codes[:].bitcast(FP8X4),
+                    rhs_scale=scales[:],
+                    start=True,
+                    stop=True,
+                )
+
+        first_product(xc_first, 0)
+        vs_picked_scales = keep.tile([P, N], U8, name="vs_picked_scales", tag="xc_first", align_bytes=64)
+        nc.vector.tensor_copy(out=vs_picked_scales[:], in_=vs_spread[:].indirect(store_list[:]))
+        first_product(xc_second, 1)
+
         for h in (0, 1):
-            for t in early:
-                a_sb = keep.tile([P, HALF], F32, name=f"a{t}{h}_sb")
-                nc.scalar.copy(out=a_sb[:], in_=half_banks[t, h][:])
-                scatter(t, a_sb, h * HALF, HALF)
-        for t in late:
-            a_sb = keep.tile([P, J], F32, name=f"a{t}_sb", tag=f"a{t}_sb", align_bytes=64)
-            nc.scalar.copy(out=a_sb[:], in_=whole_banks[t][:])
-            scatter(t, a_sb, 0, J)
+            for t in EARLY:
+                a_half = keep.tile([P, HALF], F32, name=f"a{t}{h}_sb")
+                nc.scalar.copy(out=a_half[:], in_=half_banks[t, h][:])
+                nc.vector.tensor_copy(out=pw[t][:].indirect(entries(board_list, h * HALF, HALF)), in_=a_half[:])
+        for t in LATE:
+            a_whole = keep.tile([P, J], F32, name=f"a{t}_sb", tag=f"a{t}_sb", align_bytes=64)
+            nc.scalar.copy(out=a_whole[:], in_=whole_banks[t][:])
+            nc.vector.tensor_copy(out=pw[t][:].indirect(entries(board_list, 0, J)), in_=a_whole[:])
 
         vs_picked = keep.tile([P, N], U32, name="vs_picked", tag="a3_sb", align_bytes=64)
-        nc.vector.tensor_copy(out=vs_picked[:], in_=vs_raw[:].indirect(l7[:]))
+        nc.vector.tensor_copy(out=vs_picked[:], in_=vs_raw[:].indirect(store_list[:]))
 
         pg = [keep.tile([P, S], F32, name=f"pg{t}") for t in range(PACK)]
         for t in range(PACK):
             own = keep.tile([P, S], F32, name=f"own{t}")
             shared = keep.tile([P, S], F32, name=f"shared{t}")
-            nc.scalar.activation(out=own[:], in_=pw[t][:].indirect(l4[:]), func=COPY, scale=sa_sb[:, t : t + 1])
-            nc.scalar.activation(out=shared[:], in_=pw[t][:].indirect(l5[:]), func=COPY, scale=sb_sb[:, t : t + 1])
+            scaled_gather(own[:], pw[t], own_list[:], sa_sb, t)
+            scaled_gather(shared[:], pw[t], shared_list[:], sb_sb, t)
             nc.vector.tensor_tensor(out=pg[t][:], in0=own[:], in1=shared[:], op=MAX)
+
         hid = keep.tile([P, PACK, O], BF16, name="hid")
-
-        def read_places(t, first, count):
-            nc.scalar.activation(
-                out=hid[:, t, first : first + count],
-                in_=pg[t][:].indirect(l6[:, first // 16 : (first + count) // 16]),
-                func=COPY,
-                scale=sd_sb[:, t : t + 1],
-            )
-
         for t in range(PACK - 1):
-            read_places(t, 0, O)
+            scaled_gather(hid[:, t, :], pg[t], entries(place_list, 0, O), sd_sb, t)
         grouped_hid = keep.tile([P, O, PACK], BF16, name="grouped_hid", align_bytes=64)
         hid_codes = keep.tile([P, O], U32, name="hid_codes", align_bytes=64)
         hid_scales = keep.tile([P, O], U8, name="hid_scales", align_bytes=64)
-        halves = [slice(0, O // 2), slice(O // 2, O)]
-        for cols in halves:
-            read_places(PACK - 1, cols.start, O // 2)
-            nc.vector.tensor_copy(
-                out=grouped_hid[:, cols, :].rearrange("p (c i) t -> p c t i", i=4),
-                in_=hid[:, :, cols].rearrange("p t (c i) -> p c t i", i=4),
+        place_halves = [slice(0, O // 2), slice(O // 2, O)]
+        for places in place_halves:
+            scaled_gather(
+                hid[:, PACK - 1, places], pg[PACK - 1], entries(place_list, places.start, O // 2), sd_sb, PACK - 1
             )
-        for cols in halves:
-            nc.vector.quantize_mx(
-                out=hid_codes[:, cols].bitcast(FP8X4),
-                scales=hid_scales[:, cols],
-                in_=grouped_hid[:, cols, :].rearrange("p c t -> p (c t)"),
-            )
+            interleave(grouped_hid[:, places, :], hid[:, :, places])
+        for places in place_halves:
+            quantize(hid_codes[:, places], hid_scales[:, places], grouped_hid[:, places, :])
 
-        for i in range(N // P):
-            cols = slice(i * P, (i + 1) * P)
+        ways_out = [(nc.vector.tensor_copy, nc.sync), (nc.scalar.copy, nc.scalar)]
+        for i, (copy_out, queue) in enumerate(ways_out):
+            features = slice(i * P, (i + 1) * P)
             bank = psum.tile([P, O], F32, name=f"y{i}")
             nc.tensor.matmul_mx(
                 out=bank[:],
-                lhsT=vs_picked[:, cols].bitcast(FP8X4),
-                lhsT_scale=vs_picked_scales[:, cols],
+                lhsT=vs_picked[:, features].bitcast(FP8X4),
+                lhsT_scale=vs_picked_scales[:, features],
                 rhs=hid_codes[:].bitcast(FP8X4),
                 rhs_scale=hid_scales[:],
                 start=True,
                 stop=True,
             )
             y_sb = keep.tile([P, O], F32, name=f"y{i}_sb")
-            if i == 0:
-                nc.vector.tensor_copy(out=y_sb[:], in_=bank[:])
-                nc.sync.dma_start(out=out[cols, :], in_=y_sb[:])
-            else:
-                nc.scalar.copy(out=y_sb[:], in_=bank[:])
-                nc.scalar.dma_start(out=out[cols, :], in_=y_sb[:])
+            copy_out(out=y_sb[:], in_=bank[:])
+            queue.dma_start(out=out[features, :], in_=y_sb[:])

from contextlib import ExitStack

import concourse.mybir as mybir

K, J, R, T, U, C, O, S, N, Z = 512, 256, 512, 1024, 512, 512, 128, 256, 256, 1024
FLOPS = 2 * K * R * J + 2 * R * N * O

F32 = mybir.dt.float32
BF16 = mybir.dt.bfloat16
I32 = mybir.dt.int32
U32 = mybir.dt.uint32
U16 = mybir.dt.uint16
U8 = mybir.dt.uint8
FP8X4 = mybir.dt.float8_e4m3fn_x4
FP4X4 = mybir.dt.float4_e2m1fn_x4
COPY = mybir.ActivationFunctionType.Copy
MAX = mybir.AluOpType.max

P = 128
PACK = 4
QUADRANTS = 4
PER_COLUMN = 16
HALF = J // 2
RUN = 4
EARLY = (0, 1)
LATE = (2, 3)


def tile_picked_respelled_plain_one_ladder_store_plain_kernel(
    tc, ta, ga, gb, w_words, w_scales, sa, sb, sd, vs_words, vs_scales,
    offs, offs2, offs3, offs4, offs5, offs6, offs7, out,
):
    nc = tc.nc
    with ExitStack() as ctx:
        lists = ctx.enter_context(tc.tile_pool(name="lists", bufs=1))
        keep = ctx.enter_context(tc.tile_pool(name="keep", bufs=1))
        psum = ctx.enter_context(tc.psum_pool(name="psum", bufs=1))

        def load_list(src, name):
            tile = lists.tile(list(src.shape), U16, name=name)
            nc.sync.dma_start(tile[:], src)
            return tile

        def entries(list_tile, first, count):
            return list_tile[:, first // PER_COLUMN : (first + count) // PER_COLUMN]

        def load_factor(queue, src, name):
            tile = keep.tile([P, PACK], F32, name=name)
            queue.dma_start(out=tile[:], in_=src.rearrange("(p t) one -> p (t one)", t=PACK))
            return tile

        def load_scale_rows(src, width, name):
            rows = keep.tile([PACK, QUADRANTS, width // 4], I32, name=name)
            nc.scalar.dma_start(out=rows[:], in_=src[0].bitcast(I32).rearrange("(q r) n -> r q n", r=PACK))
            return rows

        def spread_scale_rows(rows, width, name):
            spread = keep.tile([P, width], U8, name=name, align_bytes=64)
            nc.vector.memset(spread[:].bitcast(I32), 0)
            for q in range(QUADRANTS):
                nc.vector.tensor_copy(out=spread[32 * q : 32 * q + PACK, :].bitcast(I32), in_=rows[:, q, :])
            return spread

        def interleave(grouped, planes):
            nc.vector.tensor_copy(
                out=grouped.rearrange("p (c i) t -> p c t i", i=RUN),
                in_=planes.rearrange("p t (c i) -> p c t i", i=RUN),
            )

        def quantize(codes, scales, grouped):
            nc.vector.quantize_mx(out=codes.bitcast(FP8X4), scales=scales, in_=grouped.rearrange("p c t -> p (c t)"))

        def scaled_gather(dst, window, offsets, factor, t):
            nc.scalar.activation(out=dst, in_=window[:].indirect(offsets), func=COPY, scale=factor[:, t : t + 1])

        ta_planes = ta.rearrange("(p t) c -> t p c", t=PACK)

        def load_ta(t):
            tile = keep.tile([P, T], F32, name=f"ta{t}", tag=f"ta{t}", align_bytes=64)
            nc.sync.dma_start(out=tile[:], in_=ta_planes[t])
            return tile

        warm_in = keep.tile([P, 1], F32, name="warm_in")
        warm_out = keep.tile([P, 1], F32, name="warm_out")
        nc.vector.memset(warm_in[:], 0.0)
        nc.scalar.activation(out=warm_out[:], in_=warm_in[:], func=COPY)

        ta_sb = [load_ta(0)]
        word_list = load_list(offs, "word_list")
        ga_sb = load_factor(nc.scalar, ga, "ga_sb")
        w_rows = load_scale_rows(w_scales, R, "w_rows")
        vs_rows = load_scale_rows(vs_scales, Z, "vs_rows")
        gb_sb = load_factor(nc.gpsimd, gb, "gb_sb")
        ta_sb.extend([load_ta(1), load_ta(2)])
        slot_list = load_list(offs2, "slot_list")
        ta_sb.append(load_ta(3))
        w_raw = keep.tile([P, 2 * R], U8, name="w_raw")
        nc.sync.dma_start(out=w_raw[:], in_=w_words[0])
        store_list = load_list(offs7, "store_list")
        board_list = load_list(offs3, "board_list")
        own_list = load_list(offs4, "own_list")
        shared_list = load_list(offs5, "shared_list")
        sa_sb = load_factor(nc.sync, sa, "sa_sb")
        sb_sb = load_factor(nc.sync, sb, "sb_sb")
        place_list = load_list(offs6, "place_list")
        sd_sb = load_factor(nc.sync, sd, "sd_sb")
        vs_raw = keep.tile([P, Z], U32, name="vs_raw")
        nc.sync.dma_start(out=vs_raw[:].bitcast(I32), in_=vs_words[0].rearrange("p n t -> p (n t)").bitcast(I32))

        pw = [keep.tile([P, C], F32, name=f"pw{t}") for t in range(PACK)]
        for t in range(PACK):
            nc.vector.memset(pw[t][:], 0.0)

        w_spread = spread_scale_rows(w_rows, R, "w_spread")
        w_dealt = keep.tile([P, 2 * R], U8, name="w_dealt", align_bytes=64)
        nc.vector.tensor_copy(
            out=w_dealt[:].bitcast(U16).rearrange("p (t c i) -> p c t i", t=PACK, i=8),
            in_=w_raw[:].bitcast(U16).rearrange("p (c i t) -> p c t i", t=PACK, i=8),
        )
        w_dealt_scales = keep.tile([P, R], U8, name="w_dealt_scales", align_bytes=64)
        nc.vector.tensor_copy(
            out=w_dealt_scales[:].rearrange("p (t c i) -> p c t i", t=PACK, i=16),
            in_=w_spread[:].rearrange("p (c i t) -> p c t i", t=PACK, i=16),
        )
        vs_spread = spread_scale_rows(vs_rows, Z, "vs_spread")

        xcd = [keep.tile([P, U], F32, name=f"xcd{t}") for t in range(PACK)]
        for t in range(PACK):
            scaled_gather(xcd[t][:], ta_sb[t], word_list[:], ga_sb, t)
        xc_first = keep.tile([P, PACK, HALF], BF16, name="xc_first", tag="xc_first", align_bytes=64)
        for t in range(PACK):
            scaled_gather(xc_first[:, t, :], xcd[t], entries(slot_list, 0, HALF), gb_sb, t)

        half_banks = {(t, h): psum.tile([P, HALF], F32, name=f"a{t}{h}") for t in EARLY for h in (0, 1)}
        whole_banks = {t: psum.tile([P, J], F32, name=f"a{t}") for t in LATE}

        xc_second = keep.tile([P, PACK, HALF], BF16, name="xc_second", tag="ta3", align_bytes=64)
        for t in range(PACK):
            scaled_gather(xc_second[:, t, :], xcd[t], entries(slot_list, HALF, HALF), gb_sb, t)

        def first_product(xc_half, h):
            grouped = keep.tile([P, HALF, PACK], BF16, name=f"grouped{h}", tag="grouped", align_bytes=64)
            interleave(grouped[:], xc_half[:])
            codes = keep.tile([P, HALF], U32, name=f"xq{h}_codes", align_bytes=64)
            scales = keep.tile([P, HALF], U8, name=f"xq{h}_scales", align_bytes=64)
            quantize(codes[:], scales[:], grouped[:])
            for t in EARLY + LATE:
                nc.tensor.matmul_mx(
                    out=half_banks[t, h][:] if t in EARLY else whole_banks[t][:, h * HALF : (h + 1) * HALF],
                    lhsT=w_dealt[:, 2 * P * t : 2 * P * (t + 1)].bitcast(FP4X4),
                    lhsT_scale=w_dealt_scales[:, P * t : P * (t + 1)],
                    rhs=codes[:].bitcast(FP8X4),
                    rhs_scale=scales[:],
                    start=True,
                    stop=True,
                )

        first_product(xc_first, 0)
        vs_picked_scales = keep.tile([P, N], U8, name="vs_picked_scales", tag="xc_first", align_bytes=64)
        nc.vector.tensor_copy(out=vs_picked_scales[:], in_=vs_spread[:].indirect(store_list[:]))
        first_product(xc_second, 1)

        for h in (0, 1):
            for t in EARLY:
                a_half = keep.tile([P, HALF], F32, name=f"a{t}{h}_sb")
                nc.scalar.copy(out=a_half[:], in_=half_banks[t, h][:])
                nc.vector.tensor_copy(out=pw[t][:].indirect(entries(board_list, h * HALF, HALF)), in_=a_half[:])
        for t in LATE:
            a_whole = keep.tile([P, J], F32, name=f"a{t}_sb", tag=f"a{t}_sb", align_bytes=64)
            nc.scalar.copy(out=a_whole[:], in_=whole_banks[t][:])
            nc.vector.tensor_copy(out=pw[t][:].indirect(entries(board_list, 0, J)), in_=a_whole[:])

        vs_picked = keep.tile([P, N], U32, name="vs_picked", tag="a3_sb", align_bytes=64)
        nc.vector.tensor_copy(out=vs_picked[:], in_=vs_raw[:].indirect(store_list[:]))

        pg = [keep.tile([P, S], F32, name=f"pg{t}") for t in range(PACK)]
        for t in range(PACK):
            own = keep.tile([P, S], F32, name=f"own{t}")
            shared = keep.tile([P, S], F32, name=f"shared{t}")
            scaled_gather(own[:], pw[t], own_list[:], sa_sb, t)
            scaled_gather(shared[:], pw[t], shared_list[:], sb_sb, t)
            nc.vector.tensor_tensor(out=pg[t][:], in0=own[:], in1=shared[:], op=MAX)

        hid = keep.tile([P, PACK, O], BF16, name="hid")
        for t in range(PACK - 1):
            scaled_gather(hid[:, t, :], pg[t], entries(place_list, 0, O), sd_sb, t)
        grouped_hid = keep.tile([P, O, PACK], BF16, name="grouped_hid", align_bytes=64)
        hid_codes = keep.tile([P, O], U32, name="hid_codes", align_bytes=64)
        hid_scales = keep.tile([P, O], U8, name="hid_scales", align_bytes=64)
        place_halves = [slice(0, O // 2), slice(O // 2, O)]
        for places in place_halves:
            scaled_gather(
                hid[:, PACK - 1, places], pg[PACK - 1], entries(place_list, places.start, O // 2), sd_sb, PACK - 1
            )
            interleave(grouped_hid[:, places, :], hid[:, :, places])
        for places in place_halves:
            quantize(hid_codes[:, places], hid_scales[:, places], grouped_hid[:, places, :])

        ways_out = [(nc.vector.tensor_copy, nc.sync), (nc.scalar.copy, nc.scalar)]
        for i, (copy_out, queue) in enumerate(ways_out):
            features = slice(i * P, (i + 1) * P)
            bank = psum.tile([P, O], F32, name=f"y{i}")
            nc.tensor.matmul_mx(
                out=bank[:],
                lhsT=vs_picked[:, features].bitcast(FP8X4),
                lhsT_scale=vs_picked_scales[:, features],
                rhs=hid_codes[:].bitcast(FP8X4),
                rhs_scale=hid_scales[:],
                start=True,
                stop=True,
            )
            y_sb = keep.tile([P, O], F32, name=f"y{i}_sb")
            copy_out(out=y_sb[:], in_=bank[:])
            queue.dma_start(out=out[features, :], in_=y_sb[:])
